import numpy as np, ml_dtypes
CORES = [2,3,42,43,82,83,122,123]
N = 8
import mx_ref
BF = ml_dtypes.bfloat16
def cols(t, e):
    v = np.concatenate([t.reshape(128, -1, 4), np.zeros((128, 1, 4), BF)], axis=1)
    return np.ascontiguousarray(v[:, e]).reshape(128, -1)
def f(rng, *shape):
    return mx_ref.flush((rng.standard_normal(shape, dtype=np.float32) * np.exp2(rng.integers(-2, 3, shape[:-1] + (1,)))).astype(BF))
def wide(rng, *shape, cols=0):
    v = rng.standard_normal(shape, dtype=np.float32) * np.exp2(rng.integers(-12, 13, shape)).astype(np.float32)
    if cols: v *= np.repeat(np.exp2(rng.integers(-cols, cols + 1, shape[:-2] + (1, shape[-1] // 4))) * (rng.random(shape[:-2] + (1, shape[-1] // 4)) > 0.0625), 4, axis=-1).astype(np.float32)
    return mx_ref.flush(v.astype(BF))
T, G, C = 256, 8, 16
def lean(rng, d, sizes):
    p, t = rng.integers(0, 128), rng.integers(0, 4)
    q, v = np.array(d["qw"]), np.array(d["x"])
    q[:, p, t::4] = BF(128)
    v[:, p, t::4] = np.repeat(np.asarray(sizes, np.float32), 16).astype(BF)
    return {"qw": q, "x": v}
def setup_inputs(rng):
    return {"qw": f(rng, N, 128, 512), "x": f(rng, N, 128, 4 * T)}
def setup_inputs_ties(rng):
    d = setup_inputs(rng); v = []
    for s in range(N):
        k = rng.permutation(np.arange(C) // 4)
        v.append(cols(d["x"][s], np.concatenate([16 * c + rng.permutation(16) for c in k])))
    d["x"] = np.stack(v); return d
def setup_inputs_last(rng):
    return lean(rng, setup_inputs(rng), [0] * (C - 1) + [128])
def setup_inputs_alike(rng):
    d = setup_inputs(rng); d["qw"] = np.concatenate([d["qw"][:, :, :64]] * G, axis=2); return d
def setup_inputs_below(rng):
    return lean(rng, setup_inputs(rng), [-128 * 4096] * C)
def setup_inputs_spread(rng):
    d = setup_inputs(rng); d["x"] = wide(rng, N, 128, 4 * T); return d
def check_inputs(d):
    b = []
    for k in ("qw", "x"):
        a = np.abs(np.asarray(d[k]).astype(np.float32))
        if not ((a == 0) | ((a >= 2.0 ** -30) & (a <= 2.0 ** 30))).all(): b.append(k)
    return b
def decode(q, n):
    out = np.zeros((128, 4 * n), np.float32)
    for b in range(4):
        e = np.zeros((128, 128, 4), np.float32); e[np.arange(128), np.arange(128), b] = 1
        out[:, b::4] = mx_ref.matmul(mx_ref.quantize(e.reshape(128, 512).astype(BF)), q)
    return out
def reference(qw, x):
    W = [mx_ref.quantize(qw[r]) for r in range(N)]
    X = [mx_ref.quantize(x[s]) for s in range(N)]
    R = [mx_ref.quantize((x[s].astype(np.float32) - decode(X[s], T)).astype(BF)) for s in range(N)]
    y = np.zeros((N, 128, N * G * 16), np.float32); ch = np.zeros((N, G, N), np.float32)
    for r in range(N):
        for s in range(N):
            a, b = mx_ref.matmul(W[r], X[s]), mx_ref.matmul(W[r], R[s])
            best = a.reshape(G, 16, C, 16).max(axis=(1, 3)).argmax(axis=1)
            ch[r][:, s] = best
            for g in range(G):
                i, j = 16 * (s * G + g), 16 * int(best[g])
                y[r][:, i:i + 16] = a[:, j:j + 16] + b[:, j:j + 16]
    return {"y": y, "ch": ch}

@@ -1,0 +1,386 @@
+from concourse.bass import DstId, RemoteDMATransfer
+from concourse.mybir import dt, AluOpType, ActivationFunctionType, AxisListType
+
+NR, Q, IT = 8, 128, 256
+LOW = -5.0e29
+NB = 3
+
+SCRATCH = {
+    "qt": ("sbuf", [128, 4 * Q], "bfloat16"),
+    "xr": ("sbuf", [128, 8 * IT], "bfloat16"),
+    "onb": ("sbuf", [128, 516], "bfloat16"),
+    "onf": ("sbuf", [128, 128], "float32"),
+    "zt": ("sbuf", [128, 516], "bfloat16"),
+    "ident": ("sbuf", [128, 128], "float32"),
+    "pm": ("sbuf", [128, 128], "float32"),
+    "rst": ("sbuf", [128, 256], "float32"),
+    "neg": ("sbuf", [128, 256], "float32"),
+    "eq": ("sbuf", [128, 512], "float8_e4m3fn_x4"),
+    "es": ("sbuf", [128, 512], "uint8"),
+    "wq": ("sbuf", [128, NR * Q], "float8_e4m3fn_x4"),
+    "ws": ("sbuf", [128, NR * Q], "uint8"),
+    "xq": ("sbuf", [128, 2 * IT], "float8_e4m3fn_x4"),
+    "xs": ("sbuf", [128, 2 * IT], "uint8"),
+    "pq": ("sbuf", [128, 2 * IT], "float8_e4m3fn_x4"),
+    "ps": ("sbuf", [128, 2 * IT], "uint8"),
+    "S": ("sbuf", [128, 2048], "float32"),
+    "P": ("sbuf", [128, 1024], "float32"),
+    "lt": ("sbuf", [128, 64], "float32"),
+    "cc": ("sbuf", [128, 16], "float32"),
+    "bc": ("sbuf", [128, 512], "float32"),
+    "of": ("sbuf", [128, 256], "uint16"),
+    "gt": ("sbuf", [128, 6 * 1024], "bfloat16"),
+    "cq": ("sbuf", [128, 6 * 256], "float8_e4m3fn_x4"),
+    "cs": ("sbuf", [128, 6 * 256], "uint8"),
+    "lq": ("sbuf", [128, NR * 256], "float8_e4m3fn_x4"),
+    "ls": ("sbuf", [128, NR * 256], "uint8"),
+    "ab": ("sbuf", [128, 512], "float32"),
+    "yt": ("sbuf", [128, 1024], "float32"),
+    "cht": ("sbuf", [32, 32], "float32"),
+    "chu": ("sbuf", [32, 32], "float32"),
+    "cho": ("sbuf", [32, 8], "float32"),
+    "nb": ("dram", [1, 128, 1], "float32"),
+    "nl": ("dram", [NR, 128, 1], "float32"),
+    "sc0": ("psum", [128, 512], "float32"),
+    "sc1": ("psum", [128, 512], "float32"),
+    "tr": ("psum", [128, 512], "float32"),
+    "ob": ("psum", [128, 512], "float32"),
+    "y0": ("psum", [128, 512], "float32"),
+    "y1": ("psum", [128, 512], "float32"),
+    "y2": ("psum", [128, 512], "float32"),
+    "y3": ("psum", [128, 512], "float32"),
+}
+SEMAPHORES = (
+    ["ldq", "ldx", "kone", "ms", "mz", "kz", "kid", "kpm", "eqd", "wqd", "xqd", "rs", "rq", "lsem", "pa", "nm",
+     "nz", "nd", "ct", "sf", "sc", "sy", "hw", "fa0", "fa1", "fb", "fg", "ch1", "ch2"]
+    + ["dm%d" % b for b in range(4)]
+    + ["%s%d" % (k, b) for b in range(4) for k in ("mma", "mmb", "saa", "sab", "trd", "s2", "ltd", "cb", "bcd", "obd", "ofd")]
+    + ["%s%d" % (k, i) for i in range(6) for k in ("gx", "gr", "qz", "fm", "fy")]
+    + ["w%d" % r for r in range(NR)] + ["c%d" % r for r in range(NR)] + ["hc%d" % i for i in range(6)]
+)
+
+
+def w_relay(b, same):
+    return b == 2 or (b == 1 and not same)
+
+
+def c_relay(b, same):
+    return b == 0 or (b == 1 and not same)
+
+
+def rank_program(g, core, T, topo):
+    cores = list(T.cores)
+    groups, chips = [], []
+    for r in range(len(cores)):
+        c = topo.chip(cores[r])
+        if c not in chips:
+            chips.append(c)
+            groups.append([])
+        groups[chips.index(c)].append(r)
+    ng = len(groups)
+    place = {}
+    for k in range(ng):
+        for j in range(len(groups[k])):
+            place[groups[k][j]] = (k, j)
+    step = sorted(range(1, ng), key=lambda d: topo.same_plane(chips[0], chips[d]))
+
+    def helper_of(r):
+        own = cores[r]
+        far = [c for c in topo.cores_of(own) if topo.die(c) != topo.die(own) and T.rank_of(c) is None
+               and all(topo.may_write(c, t) for t in cores)]
+        return far[place[r][1]]
+
+    def w_targets(r):
+        k, j = place[r]
+        return [[(s, w_relay(b, place[s][1] == j)) for s in groups[(k + step[b]) % ng]] for b in range(NB)]
+
+    def c_targets(s):
+        k, j = place[s]
+        out = []
+        for b in range(NB):
+            l = [(r, c_relay(b, place[r][1] == j)) for r in groups[(k - step[b]) % ng]]
+            out.append(sorted(l, key=lambda e: not e[1]))
+        return out
+
+    queue = {"g": g, "v": g.vector, "s": g.scalar, "t": g.tensor, "y": g.sync}
+    cnt, seen, top = {}, {}, {}
+
+    def inc(ins, name, k=1):
+        ins.then_inc(T.sem[name], k)
+        cnt[name] = cnt.get(name, 0) + k
+
+    def wait(q, name):
+        v = cnt[name]
+        if seen.get((q, name), 0) < v:
+            queue[q].wait_ge(T.sem[name], v)
+            seen[(q, name)] = v
+            top[name] = max(top.get(name, 0), v)
+
+    def expect(name, k):
+        cnt[name] = cnt.get(name, 0) + k
+
+    def finish():
+        for name in cnt:
+            if top.get(name, 0) < cnt[name]:
+                wait("g", name)
+
+    far_core = [c for c in cores if topo.chip(c) != topo.chip(core)][0]
+    offe = topo.engines(core, far_core)
+
+    def mask_to(dst):
+        if topo.chip(dst) != topo.chip(core):
+            return topo.mask(core, dst)
+        return sum(1 << e for e in topo.engines(core, dst) if e not in offe)
+
+    def send(dsts, src, dst, sem, mask=None):
+        m = mask_to(dsts[0]) if mask is None else mask
+        if len(dsts) == 1:
+            rid, pid, _ = topo.addr(dsts[0])
+            g.remote_dma(out_ap=dst, in_ap=src, remote_sem=T.sem[sem], local_sem=T.sem["lsem"], pid=pid,
+                         routing_id=rid, dma_engine_mask=m)
+        else:
+            ids = []
+            for d in dsts:
+                rid, pid, _ = topo.addr(d)
+                ids.append(DstId(rid=rid, pnc=pid))
+            g.remote_dma_fused([RemoteDMATransfer(dst_ids=ids, dma_engine_mask=m, remote_sem=T.sem[sem], srcs=[src],
+                                                  dsts=[dst] * len(dsts))], local_sem=T.sem["lsem"])
+        cnt["lsem"] = cnt.get("lsem", 0) + bin(m).count("1")
+
+    n_off, n_on = len(offe), len([e for e in topo.engines(core, [c for c in topo.cores_of(core) if c != core][0])
+                                  if e not in offe])
+
+    def send_w(dsts, r, sem):
+        send(dsts, T.wq[:, Q * r:Q * r + Q].bitcast(dt.uint8), T.wq[:, Q * r:Q * r + Q].bitcast(dt.uint8), sem)
+        send(dsts, T.ws[:, Q * r:Q * r + Q], T.ws[:, Q * r:Q * r + Q], sem)
+
+    def send_c(dst, i, s):
+        send([dst], T.cq[:, 256 * i:256 * i + 256].bitcast(dt.uint8), T.lq[:, 256 * s:256 * s + 256].bitcast(dt.uint8), "c%d" % s)
+        send([dst], T.cs[:, 256 * i:256 * i + 256], T.ls[:, 256 * s:256 * s + 256], "c%d" % s)
+
+    rank = T.rank_of(core)
+    if rank is None:
+        mine = [r for r in range(len(cores)) if helper_of(r) == core]
+        if not mine:
+            return
+        r = mine[0]
+        relayed = [[s for s, rel in l if rel] for l in w_targets(r)]
+        if any(relayed):
+            expect("hw", 2 * n_on)
+            wait("g", "hw")
+            for l in relayed:
+                if l:
+                    send_w([cores[s] for s in l], r, "w%d" % r)
+        for b, l in enumerate(c_targets(r)):
+            for j, (d, rel) in enumerate(l):
+                if rel:
+                    i = 2 * b + j
+                    expect("hc%d" % i, 2 * n_on)
+                    wait("g", "hc%d" % i)
+                    send_c(cores[d], i, r)
+        finish()
+        return
+
+    m, _ = place[rank]
+    duo = groups[m]
+    mate = [r for r in duo if r != rank][0]
+    helper = helper_of(rank)
+    v, pe, act, sy = g.vector, g.tensor, g.scalar, g.sync
+    COPY = ActivationFunctionType.Copy
+    ADD, MAX = AluOpType.add, AluOpType.max
+
+    inc(sy.dma_start(T.qt[:, :], T.qw[:, :]), "ldq", 16)
+    inc(act.dma_start(T.xr[:, 0:4 * IT], T.x[:, :]), "ldx", 16)
+
+    inc(v.memset(T.onb[:, :], 1.0), "kone")
+    inc(v.memset(T.onf[:, :], 1.0), "kone")
+    inc(v.memset(T.rst[:, :], 0.0), "mz")
+    inc(v.memset(T.bc[:, :], 0.0), "ms")
+    inc(v.memset(T.neg[:, :], LOW), "ms")
+    inc(v.memset(T.cht[:, :], 0.0), "ms")
+    wait("v", "mz")
+    inc(v.memset(T.rst[:, 0:256:16], LOW), "ms")
+    wait("g", "kone")
+    inc(g.affine_select(T.zt[:, :], T.onb[:, :], [[-1, 516]], AluOpType.is_equal, 0.0, 3, 4), "kz")
+
+    wait("v", "ldq")
+    inc(v.quantize_mx(T.wq[:, Q * rank:Q * rank + Q], T.ws[:, Q * rank:Q * rank + Q], T.qt[:, :]), "wqd")
+    wait("g", "wqd")
+    targets = w_targets(rank)
+    relayed_any = any(rel for l in targets for _, rel in l)
+    for b, l in enumerate(targets):
+        direct = [cores[s] for s, rel in l if not rel]
+        if direct:
+            send_w(direct, rank, "w%d" % rank)
+        if b == 0 and relayed_any:
+            send_w([helper], rank, "hw")
+    inc(g.affine_select(T.ident[:, :], T.onf[:, :], [[-1, 128]], AluOpType.is_equal, 0.0, 0, 1), "kid")
+    inc(g.iota(T.pm[:, :], [[0, 8], [1, 16]], 0, 0, allow_small_or_imprecise_dtypes=True), "kpm")
+
+    wait("v", "ldx")
+    inc(v.quantize_mx(T.xq[:, 0:IT], T.xs[:, 0:IT], T.xr[:, 0:4 * IT]), "xqd")
+    wait("v", "kz")
+    for b in range(4):
+        inc(v.quantize_mx(T.eq[:, 128 * b:128 * b + 128], T.es[:, 128 * b:128 * b + 128], T.zt[:, 3 - b:3 - b + 512]), "eqd")
+    wait("t", "xqd")
+    wait("t", "eqd")
+    ybank = [T.y0, T.y1, T.y2, T.y3]
+    for b in range(4):
+        inc(pe.matmul_mx(ybank[b][:, 0:IT], T.eq[:, 128 * b:128 * b + 128], T.es[:, 128 * b:128 * b + 128],
+                         T.xq[:, 0:IT], T.xs[:, 0:IT], True, True), "dm%d" % b)
+    for b in range(4):
+        wait("v", "dm%d" % b)
+        inc(v.tensor_tensor(T.xr[:, 4 * IT + b:8 * IT:4], T.xr[:, b:4 * IT:4], ybank[b][:, 0:IT], AluOpType.subtract), "rs")
+    wait("v", "rs")
+    inc(v.quantize_mx(T.xq[:, IT:2 * IT], T.xs[:, IT:2 * IT], T.xr[:, 4 * IT:8 * IT]), "rq")
+    wait("g", "rq")
+    send([cores[mate]], T.xq[:, :].bitcast(dt.uint8), T.pq[:, :].bitcast(dt.uint8), "pa")
+    send([cores[mate]], T.xs[:, :], T.ps[:, :], "pa")
+
+    wait("y", "ms")
+    inc(sy.dma_start(T.nb[0:1, :, 0], T.bc[64:65, 0:128]), "nz", 16)
+    wait("y", "nz")
+
+    def choose(b):
+        o, p = 512 * b, 256 * b
+        wait("t", "kid")
+        if b:
+            wait("t", "s2%d" % (b - 1))
+        for h in range(2):
+            wait("t", ("saa%d", "sab%d")[h] % b)
+            inc(pe.transpose(T.tr[0:16, 128 * h:128 * h + 128], T.S[:, o + 256 * h + 15:o + 256 * h + 256:16], T.ident[:, :]), "trd%d" % b)
+        wait("v", "trd%d" % b)
+        inc(v.tensor_tensor_scan(T.P[0:16, p:p + 256], T.tr[0:16, 0:256], T.neg[0:16, :], LOW, MAX, MAX), "s2%d" % b)
+        wait("v", "s2%d" % b)
+        inc(v.tensor_scalar(T.lt[0:16, 16 * b:16 * b + 16], T.P[0:16, p + 15:p + 256:16], T.P[0:16, p + 255:p + 256], 64.0,
+                            AluOpType.is_lt, AluOpType.mult), "ltd%d" % b)
+        wait("v", "ltd%d" % b)
+        inc(v.tensor_reduce(T.cc[0:16, 4 * b:4 * b + 1], T.lt[0:16, 16 * b:16 * b + 16], AxisListType.X, ADD), "cb%d" % b)
+        wait("v", "cb%d" % b)
+        wait("v", "kpm")
+        col = T.cc[0:16, 4 * b:4 * b + 1]
+        if b < NB:
+            inc(v.tensor_scalar(T.bc[0:16, 128 * b:128 * b + 128], T.pm[0:16, :], col, None, ADD), "bcd%d" % b)
+        else:
+            inc(v.tensor_scalar(T.bc[0:16, 128 * b:128 * b + 128], T.pm[0:16, :], 4.0, col, AluOpType.mult, ADD), "bcd%d" % b)
+        wait("t", "bcd%d" % b)
+        if b:
+            wait("t", "ofd%d" % (b - 1))
+        inc(pe.transpose(T.ob[:, 0:128], T.bc[:, 128 * b:128 * b + 128], T.ident[:, :]), "obd%d" % b)
+        wait("v", "obd%d" % b)
+
+    goals = c_targets(rank)
+    for b in range(NB):
+        src = groups[(m - step[b]) % ng]
+        for r in src:
+            expect("w%d" % r, 2 * n_off)
+            wait("t", "w%d" % r)
+        c0 = Q * src[0]
+        for h, bank in enumerate((T.sc0, T.sc1)):
+            if b:
+                wait("t", ("saa%d", "sab%d")[h] % (b - 1))
+            inc(pe.matmul_mx(bank[:, 0:256], T.xq[:, 128 * h:128 * h + 128], T.xs[:, 128 * h:128 * h + 128],
+                             T.wq[:, c0:c0 + 256], T.ws[:, c0:c0 + 256], True, True), ("mma%d", "mmb%d")[h] % b)
+        wait("v", "ms")
+        for h, bank in enumerate((T.sc0, T.sc1)):
+            wait("v", ("mma%d", "mmb%d")[h] % b)
+            inc(v.tensor_tensor_scan(T.S[:, 512 * b + 256 * h:512 * b + 256 * h + 256], T.rst[:, :], bank[:, 0:256], 0.0, ADD, MAX),
+                ("saa%d", "sab%d")[h] % b)
+        choose(b)
+        for u in range(4):
+            inc(v.tensor_scalar(T.of[:, 64 * b + u:64 * b + 64:4], T.ob[:, 0:16], float(16 * u), None, ADD), "ofd%d" % b)
+        wait("v", "ofd%d" % b)
+        wait("s", "ofd%d" % b)
+        wait("s", "rs")
+        for j, (r, rel) in enumerate(goals[b]):
+            i = 2 * b + j
+            f0 = 64 * b + 32 * src.index(r)
+            inc(v.tensor_copy(T.gt[:, 1024 * i:1024 * i + 512], T.xr[:, 0:1024].indirect(T.of[:, f0:f0 + 32])), "gx%d" % i)
+            inc(act.activation(T.gt[:, 1024 * i + 512:1024 * i + 1024], T.xr[:, 1024:2048].indirect(T.of[:, f0:f0 + 32]), COPY), "gr%d" % i)
+            wait("v", "gx%d" % i)
+            wait("v", "gr%d" % i)
+            inc(v.quantize_mx(T.cq[:, 256 * i:256 * i + 256], T.cs[:, 256 * i:256 * i + 256], T.gt[:, 1024 * i:1024 * i + 1024]), "qz%d" % i)
+        wait("y", "cb%d" % b)
+        inc(sy.dma_start(T.nb[0:1, 8 * src[0]:8 * src[0] + 16, 0], T.cc[0:16, 4 * b:4 * b + 1]), "nd", 16)
+        for j, (r, rel) in enumerate(goals[b]):
+            i = 2 * b + j
+            wait("g", "qz%d" % i)
+            if rel:
+                send([helper], T.cq[:, 256 * i:256 * i + 256].bitcast(dt.uint8), T.cq[:, 256 * i:256 * i + 256].bitcast(dt.uint8), "hc%d" % i)
+                send([helper], T.cs[:, 256 * i:256 * i + 256], T.cs[:, 256 * i:256 * i + 256], "hc%d" % i)
+            else:
+                send_c(cores[r], i, rank)
+            if b == NB - 1 and j == 0:
+                wait("g", "nd")
+                others = [cores[o] for k in range(ng) if k != m for o in groups[k]]
+                send(others, T.nb[0], T.nl[rank], "nm", 1 << offe[-1])
+
+    own = {rank: (T.xq, T.xs), mate: (T.pq, T.ps)}
+    wcols = T.wq[:, Q * rank:Q * rank + Q], T.ws[:, Q * rank:Q * rank + Q]
+    expect("pa", 2 * n_on)
+    b = NB
+    banks = {rank: (T.sc0, T.sc1), mate: (T.y0, T.y1)}
+    wait("t", "rs")
+    wait("t", "wqd")
+    wait("t", "rq")
+    for s in (rank, mate):
+        if s == mate:
+            wait("t", "pa")
+        for h in range(2):
+            if s == rank:
+                wait("t", ("saa%d", "sab%d")[h] % (b - 1))
+            inc(pe.matmul_mx(banks[s][h][:, 0:128], own[s][0][:, 128 * h:128 * h + 128], own[s][1][:, 128 * h:128 * h + 128],
+                             wcols[0], wcols[1], True, True), ("mma%d", "mmb%d")[h] % b)
+    for l, s in enumerate(duo):
+        bank = (T.y2, T.y3)[l]
+        pe.matmul_mx(bank[:, 0:IT], wcols[0], wcols[1], own[s][0][:, 0:IT], own[s][1][:, 0:IT], True, False)
+        inc(pe.matmul_mx(bank[:, 0:IT], wcols[0], wcols[1], own[s][0][:, IT:2 * IT], own[s][1][:, IT:2 * IT], False, True), "fa%d" % l)
+    for h in range(2):
+        wait("v", ("mma%d", "mmb%d")[h] % b)
+        for l, s in enumerate(duo):
+            o = 512 * b + 256 * h + 128 * l
+            inc(v.tensor_tensor_scan(T.S[:, o:o + 128], T.rst[:, 0:128], banks[s][h][:, 0:128], 0.0, ADD, MAX), ("saa%d", "sab%d")[h] % b)
+    for l in range(2):
+        wait("s", "fa%d" % l)
+        inc(act.activation(T.ab[:, IT * l:IT * l + IT], (T.y2, T.y3)[l][:, 0:IT], COPY), "fb")
+    choose(b)
+    inc(v.tensor_scalar(T.of[:, 64 * b:64 * b + 16], T.ob[:, 0:16], 0.25, None, AluOpType.mult), "ofd%d" % b)
+    wait("v", "ofd%d" % b)
+    wait("v", "fb")
+    for l, s in enumerate(duo):
+        f0 = 64 * b + 8 * l
+        inc(v.tensor_copy(T.yt[:, 128 * s:128 * s + 128], T.ab[:, IT * l:IT * l + IT].indirect(T.of[:, f0:f0 + 8])), "fg")
+    wait("y", "cb%d" % b)
+    inc(sy.dma_start(T.cht[duo[0]:duo[0] + 2, 0:8], T.cc[0:16, 4 * b:4 * b + 1]), "ct", 16)
+    wait("y", "fg")
+    inc(sy.dma_start(T.y[:, 128 * duo[0]:128 * duo[0] + 256], T.yt[:, 128 * duo[0]:128 * duo[0] + 256]), "sf", 16)
+
+    freed = ["saa%d" % NB, "sab%d" % NB, "fb", "fb"]
+    for b in range(NB):
+        for j, s in enumerate(groups[(m + step[b]) % ng]):
+            i = 2 * b + j
+            bank = ybank[i % 4]
+            expect("c%d" % s, 2 * n_off)
+            wait("t", freed[i] if i < 4 else "fy%d" % (i - 4))
+            wait("t", "c%d" % s)
+            pe.matmul_mx(bank[:, 0:128], wcols[0], wcols[1], T.lq[:, 256 * s:256 * s + 128], T.ls[:, 256 * s:256 * s + 128], True, False)
+            inc(pe.matmul_mx(bank[:, 0:128], wcols[0], wcols[1], T.lq[:, 256 * s + 128:256 * s + 256],
+                             T.ls[:, 256 * s + 128:256 * s + 256], False, True), "fm%d" % i)
+            wait("s", "fm%d" % i)
+            inc(act.activation(T.yt[:, 128 * s:128 * s + 128], bank[:, 0:128], COPY), "fy%d" % i)
+            wait("s", "fy%d" % i)
+            inc(act.dma_start(T.y[:, 128 * s:128 * s + 128], T.yt[:, 128 * s:128 * s + 128]), "sy", 16)
+
+    expect("nm", len(cores) - len(duo))
+    wait("y", "nm")
+    for k in range(ng):
+        if k != m:
+            s = groups[k][0]
+            inc(sy.dma_start(T.cht[s:s + 2, 0:8], T.nl[s:s + 2, 8 * rank:8 * rank + 8, 0]), "ct", 16)
+    wait("v", "ct")
+    inc(v.transpose(T.chu[:, :], T.cht[:, :]), "ch1")
+    wait("v", "ch1")
+    inc(v.tensor_scalar(T.cho[0:8, 0:8], T.chu[0:8, 0:8], 1.0 / 64.0, None, AluOpType.mult), "ch2")
+    wait("y", "ch2")
+    inc(sy.dma_start(T.ch[:, :], T.cho[0:8, 0:8]), "sc", 16)
+    finish()

@@ -4,6 +4,7 @@ from concourse.mybir import dt, AluOpType, ActivationFunctionType, AxisListType
 NR, Q, IT = 8, 128, 256
 LOW = -5.0e29
 NB = 3
+NI = 5
 
 SCRATCH = {
     "qt": ("sbuf", [128, 4 * Q], "bfloat16"),
@@ -23,22 +24,25 @@ SCRATCH = {
     "xs": ("sbuf", [128, 2 * IT], "uint8"),
     "pq": ("sbuf", [128, 2 * IT], "float8_e4m3fn_x4"),
     "ps": ("sbuf", [128, 2 * IT], "uint8"),
-    "S": ("sbuf", [128, 2048], "float32"),
+    "fq": ("sbuf", [128, 2 * IT], "float8_e4m3fn_x4"),
+    "fs": ("sbuf", [128, 2 * IT], "uint8"),
+    "S": ("sbuf", [128, 2304], "float32"),
     "P": ("sbuf", [128, 1024], "float32"),
     "lt": ("sbuf", [128, 64], "float32"),
     "cc": ("sbuf", [128, 16], "float32"),
     "bc": ("sbuf", [128, 512], "float32"),
     "of": ("sbuf", [128, 256], "uint16"),
-    "gt": ("sbuf", [128, 6 * 1024], "bfloat16"),
-    "cq": ("sbuf", [128, 6 * 256], "float8_e4m3fn_x4"),
-    "cs": ("sbuf", [128, 6 * 256], "uint8"),
+    "gt": ("sbuf", [128, NI * 1024], "bfloat16"),
+    "cq": ("sbuf", [128, NI * 256], "float8_e4m3fn_x4"),
+    "cs": ("sbuf", [128, NI * 256], "uint8"),
     "lq": ("sbuf", [128, NR * 256], "float8_e4m3fn_x4"),
     "ls": ("sbuf", [128, NR * 256], "uint8"),
-    "ab": ("sbuf", [128, 512], "float32"),
+    "ab": ("sbuf", [128, 3 * IT], "float32"),
     "yt": ("sbuf", [128, 1024], "float32"),
     "cht": ("sbuf", [32, 32], "float32"),
     "chu": ("sbuf", [32, 32], "float32"),
     "cho": ("sbuf", [32, 8], "float32"),
+    "nx": ("sbuf", [128, 1], "float32"),
     "nb": ("dram", [1, 128, 1], "float32"),
     "nl": ("dram", [NR, 128, 1], "float32"),
     "sc0": ("psum", [128, 512], "float32"),
@@ -51,21 +55,21 @@ SCRATCH = {
     "y3": ("psum", [128, 512], "float32"),
 }
 SEMAPHORES = (
-    ["ldq", "ldx", "kone", "ms", "mz", "kz", "kid", "kpm", "eqd", "wqd", "xqd", "rs", "rq", "lsem", "pa", "nm",
-     "nz", "nd", "ct", "sf", "sc", "sy", "hw", "fa0", "fa1", "fb", "fg", "ch1", "ch2"]
+    ["ldq", "ldx", "kone", "ms", "mz", "kz", "kid", "kpm", "eqd", "wqd", "xqd", "rs", "rq", "lsem", "pa", "pf", "nm", "nx",
+     "nz", "nd", "ct", "sc", "sy", "hw", "fa0", "fa1", "fa2", "fb", "fg", "ch1", "ch2", "ch3"]
     + ["dm%d" % b for b in range(4)]
     + ["%s%d" % (k, b) for b in range(4) for k in ("mma", "mmb", "saa", "sab", "trd", "s2", "ltd", "cb", "bcd", "obd", "ofd")]
-    + ["%s%d" % (k, i) for i in range(6) for k in ("gx", "gr", "qz", "fm", "fy")]
-    + ["w%d" % r for r in range(NR)] + ["c%d" % r for r in range(NR)] + ["hc%d" % i for i in range(6)]
+    + ["%s%d" % (k, i) for i in range(NI) for k in ("gx", "gr", "qz", "fm", "fy")]
+    + ["w%d" % r for r in range(NR)] + ["c%d" % r for r in range(NR)] + ["hc%d" % i for i in range(NI)]
 )
 
 
 def w_relay(b, same):
-    return b == 2 or (b == 1 and not same)
+    return b == 1 and not same
 
 
-def c_relay(b, same):
-    return b == 0 or (b == 1 and not same)
+def c_relay(b):
+    return b == 0
 
 
 def rank_program(g, core, T, topo):
@@ -84,23 +88,24 @@ def rank_program(g, core, T, topo):
             place[groups[k][j]] = (k, j)
     step = sorted(range(1, ng), key=lambda d: topo.same_plane(chips[0], chips[d]))
 
+    def peer_of(r):
+        k, j = place[r]
+        return groups[(k + step[-1]) % ng][j]
+
+    def sources(r, b):
+        return [s for s in groups[(place[r][0] - step[b]) % ng] if s != peer_of(r)]
+
+    def owners(r, b):
+        return [s for s in groups[(place[r][0] + step[b]) % ng] if s != peer_of(r)]
+
+    def w_roads(r, relay):
+        return [[s for s in owners(r, b) if w_relay(b, place[s][1] == place[r][1]) == relay] for b in range(NB)]
+
     def helper_of(r):
         own = cores[r]
         far = [c for c in topo.cores_of(own) if topo.die(c) != topo.die(own) and T.rank_of(c) is None
                and all(topo.may_write(c, t) for t in cores)]
         return far[place[r][1]]
-
-    def w_targets(r):
-        k, j = place[r]
-        return [[(s, w_relay(b, place[s][1] == j)) for s in groups[(k + step[b]) % ng]] for b in range(NB)]
-
-    def c_targets(s):
-        k, j = place[s]
-        out = []
-        for b in range(NB):
-            l = [(r, c_relay(b, place[r][1] == j)) for r in groups[(k - step[b]) % ng]]
-            out.append(sorted(l, key=lambda e: not e[1]))
-        return out
 
     queue = {"g": g, "v": g.vector, "s": g.scalar, "t": g.tensor, "y": g.sync}
     cnt, seen, top = {}, {}, {}
@@ -151,8 +156,13 @@ def rank_program(g, core, T, topo):
                                   if e not in offe])
 
     def send_w(dsts, r, sem):
-        send(dsts, T.wq[:, Q * r:Q * r + Q].bitcast(dt.uint8), T.wq[:, Q * r:Q * r + Q].bitcast(dt.uint8), sem)
-        send(dsts, T.ws[:, Q * r:Q * r + Q], T.ws[:, Q * r:Q * r + Q], sem)
+        codes, plane = T.wq[:, Q * r:Q * r + Q].bitcast(dt.uint8), T.ws[:, Q * r:Q * r + Q]
+        send(dsts, codes, codes, sem)
+        send(dsts, plane, plane, sem)
+
+    def send_xr(dst, codes, plane, codes2, plane2, sem):
+        send([dst], codes[:, :].bitcast(dt.uint8), codes2[:, :].bitcast(dt.uint8), sem)
+        send([dst], plane[:, :], plane2[:, :], sem)
 
     def send_c(dst, i, s):
         send([dst], T.cq[:, 256 * i:256 * i + 256].bitcast(dt.uint8), T.lq[:, 256 * s:256 * s + 256].bitcast(dt.uint8), "c%d" % s)
@@ -160,37 +170,38 @@ def rank_program(g, core, T, topo):
 
     rank = T.rank_of(core)
     if rank is None:
-        mine = [r for r in range(len(cores)) if helper_of(r) == core]
-        if not mine:
-            return
-        r = mine[0]
-        relayed = [[s for s, rel in l if rel] for l in w_targets(r)]
-        if any(relayed):
-            expect("hw", 2 * n_on)
-            wait("g", "hw")
-            for l in relayed:
-                if l:
-                    send_w([cores[s] for s in l], r, "w%d" % r)
-        for b, l in enumerate(c_targets(r)):
-            for j, (d, rel) in enumerate(l):
-                if rel:
-                    i = 2 * b + j
-                    expect("hc%d" % i, 2 * n_on)
-                    wait("g", "hc%d" % i)
-                    send_c(cores[d], i, r)
-        finish()
+        for r in range(len(cores)):
+            if helper_of(r) == core:
+                expect("hw", 2 * n_on)
+                wait("g", "hw")
+                for l in w_roads(r, True):
+                    if l:
+                        send_w([cores[s] for s in l], r, "w%d" % r)
+                expect("pa", 2 * n_on)
+                wait("g", "pa")
+                send_xr(cores[peer_of(r)], T.pq, T.ps, T.fq, T.fs, "pf")
+                for b in range(NB):
+                    for j, d in enumerate(sources(r, b)):
+                        if c_relay(b):
+                            i = 2 * b + j
+                            expect("hc%d" % i, 2 * n_on)
+                            wait("g", "hc%d" % i)
+                            send_c(cores[d], i, r)
+                finish()
         return
 
     m, _ = place[rank]
     duo = groups[m]
     mate = [r for r in duo if r != rank][0]
+    peer = peer_of(rank)
+    near = duo + [peer]
     helper = helper_of(rank)
     v, pe, act, sy = g.vector, g.tensor, g.scalar, g.sync
     COPY = ActivationFunctionType.Copy
     ADD, MAX = AluOpType.add, AluOpType.max
 
     inc(sy.dma_start(T.qt[:, :], T.qw[:, :]), "ldq", 16)
-    inc(act.dma_start(T.xr[:, 0:4 * IT], T.x[:, :]), "ldx", 16)
+    inc(sy.dma_start(T.xr[:, 0:4 * IT], T.x[:, :]), "ldx", 16)
 
     inc(v.memset(T.onb[:, :], 1.0), "kone")
     inc(v.memset(T.onf[:, :], 1.0), "kone")
@@ -198,24 +209,22 @@ def rank_program(g, core, T, topo):
     inc(v.memset(T.bc[:, :], 0.0), "ms")
     inc(v.memset(T.neg[:, :], LOW), "ms")
     inc(v.memset(T.cht[:, :], 0.0), "ms")
+    inc(v.memset(T.cc[:, :], 0.0), "ms")
     wait("v", "mz")
     inc(v.memset(T.rst[:, 0:256:16], LOW), "ms")
     wait("g", "kone")
     inc(g.affine_select(T.zt[:, :], T.onb[:, :], [[-1, 516]], AluOpType.is_equal, 0.0, 3, 4), "kz")
+    inc(g.affine_select(T.ident[:, :], T.onf[:, :], [[-1, 128]], AluOpType.is_equal, 0.0, 0, 1), "kid")
 
     wait("v", "ldq")
-    inc(v.quantize_mx(T.wq[:, Q * rank:Q * rank + Q], T.ws[:, Q * rank:Q * rank + Q], T.qt[:, :]), "wqd")
+    w0 = Q * rank
+    wcols = T.wq[:, w0:w0 + Q], T.ws[:, w0:w0 + Q]
+    inc(v.quantize_mx(wcols[0], wcols[1], T.qt[:, :]), "wqd")
     wait("g", "wqd")
-    targets = w_targets(rank)
-    relayed_any = any(rel for l in targets for _, rel in l)
-    for b, l in enumerate(targets):
-        direct = [cores[s] for s, rel in l if not rel]
-        if direct:
-            send_w(direct, rank, "w%d" % rank)
-        if b == 0 and relayed_any:
+    for b, l in enumerate(w_roads(rank, False)):
+        send_w([cores[s] for s in l], rank, "w%d" % rank)
+        if b == 0:
             send_w([helper], rank, "hw")
-    inc(g.affine_select(T.ident[:, :], T.onf[:, :], [[-1, 128]], AluOpType.is_equal, 0.0, 0, 1), "kid")
-    inc(g.iota(T.pm[:, :], [[0, 8], [1, 16]], 0, 0, allow_small_or_imprecise_dtypes=True), "kpm")
 
     wait("v", "ldx")
     inc(v.quantize_mx(T.xq[:, 0:IT], T.xs[:, 0:IT], T.xr[:, 0:4 * IT]), "xqd")
@@ -234,134 +243,180 @@ def rank_program(g, core, T, topo):
     wait("v", "rs")
     inc(v.quantize_mx(T.xq[:, IT:2 * IT], T.xs[:, IT:2 * IT], T.xr[:, 4 * IT:8 * IT]), "rq")
     wait("g", "rq")
-    send([cores[mate]], T.xq[:, :].bitcast(dt.uint8), T.pq[:, :].bitcast(dt.uint8), "pa")
-    send([cores[mate]], T.xs[:, :], T.ps[:, :], "pa")
+    for to in (helper, cores[mate]):
+        send_xr(to, T.xq, T.xs, T.pq, T.ps, "pa")
+    inc(g.iota(T.pm[:, :], [[0, 8], [1, 16]], 0, 0, allow_small_or_imprecise_dtypes=True), "kpm")
 
     wait("y", "ms")
     inc(sy.dma_start(T.nb[0:1, :, 0], T.bc[64:65, 0:128]), "nz", 16)
     wait("y", "nz")
 
-    def choose(b):
-        o, p = 512 * b, 256 * b
+    own = {rank: (T.xq, T.xs), mate: (T.pq, T.ps), peer: (T.fq, T.fs)}
+    banks = {rank: (T.sc0, T.sc1), mate: (T.y0, T.y1), peer: (T.y2, T.y3)}
+
+    def width(b):
+        return len(near) if b == NB else len(sources(rank, b))
+
+    def products(b):
+        if b < NB:
+            src = sources(rank, b)
+            for r in src:
+                expect("w%d" % r, 2 * n_off)
+                wait("t", "w%d" % r)
+            c0, n = Q * src[0], Q * len(src)
+            for h in range(2):
+                if b:
+                    wait("t", ("saa%d", "sab%d")[h] % (b - 1))
+                inc(pe.matmul_mx(banks[rank][h][:, 0:n], T.xq[:, 128 * h:128 * h + 128], T.xs[:, 128 * h:128 * h + 128],
+                                 T.wq[:, c0:c0 + n], T.ws[:, c0:c0 + n], True, True), ("mma%d", "mmb%d")[h] % b)
+            return
+        expect("pa", 2 * n_on)
+        expect("pf", 2 * n_off)
+        for f in ("rs", "wqd", "rq", "saa%d" % (b - 1), "sab%d" % (b - 1)):
+            wait("t", f)
+        for s in (rank, mate, peer):
+            if s != rank:
+                wait("t", "pa" if s == mate else "pf")
+            for h in range(2):
+                inc(pe.matmul_mx(banks[s][h][:, 0:128], own[s][0][:, 128 * h:128 * h + 128], own[s][1][:, 128 * h:128 * h + 128],
+                                 wcols[0], wcols[1], True, True), ("mma%d", "mmb%d")[h] % b)
+
+    def over_queries(b):
+        o, n = 512 * b, 128 * width(b)
+        wait("v", "ms")
+        for h in range(2):
+            wait("v", ("mma%d", "mmb%d")[h] % b)
+            parts = [(n, banks[rank][h], 0)] if b < NB else [(128, banks[s][h], 128 * l) for l, s in enumerate(near)]
+            for w, bank, at in parts:
+                q = o + n * h + at
+                inc(v.tensor_tensor_scan(T.S[:, q:q + w], T.rst[:, 0:w], bank[:, 0:w], 0.0, ADD, MAX), ("saa%d", "sab%d")[h] % b)
         wait("t", "kid")
         if b:
             wait("t", "s2%d" % (b - 1))
         for h in range(2):
             wait("t", ("saa%d", "sab%d")[h] % b)
-            inc(pe.transpose(T.tr[0:16, 128 * h:128 * h + 128], T.S[:, o + 256 * h + 15:o + 256 * h + 256:16], T.ident[:, :]), "trd%d" % b)
+            inc(pe.transpose(T.tr[0:n // 16, 128 * h:128 * h + 128], T.S[:, o + n * h + 15:o + n * h + n:16], T.ident[:, :]), "trd%d" % b)
+
+    def over_items(b):
+        p, k = 256 * b, 8 * width(b)
         wait("v", "trd%d" % b)
-        inc(v.tensor_tensor_scan(T.P[0:16, p:p + 256], T.tr[0:16, 0:256], T.neg[0:16, :], LOW, MAX, MAX), "s2%d" % b)
+        inc(v.tensor_tensor_scan(T.P[0:k, p:p + 256], T.tr[0:k, 0:256], T.neg[0:k, :], LOW, MAX, MAX), "s2%d" % b)
         wait("v", "s2%d" % b)
-        inc(v.tensor_scalar(T.lt[0:16, 16 * b:16 * b + 16], T.P[0:16, p + 15:p + 256:16], T.P[0:16, p + 255:p + 256], 64.0,
+        inc(v.tensor_scalar(T.lt[0:k, 16 * b:16 * b + 16], T.P[0:k, p + 15:p + 256:16], T.P[0:k, p + 255:p + 256], 64.0,
                             AluOpType.is_lt, AluOpType.mult), "ltd%d" % b)
         wait("v", "ltd%d" % b)
-        inc(v.tensor_reduce(T.cc[0:16, 4 * b:4 * b + 1], T.lt[0:16, 16 * b:16 * b + 16], AxisListType.X, ADD), "cb%d" % b)
+        col = T.cc[0:k, 4 * b:4 * b + 1]
+        inc(v.tensor_reduce(col, T.lt[0:k, 16 * b:16 * b + 16], AxisListType.X, ADD), "cb%d" % b)
         wait("v", "cb%d" % b)
         wait("v", "kpm")
-        col = T.cc[0:16, 4 * b:4 * b + 1]
         if b < NB:
-            inc(v.tensor_scalar(T.bc[0:16, 128 * b:128 * b + 128], T.pm[0:16, :], col, None, ADD), "bcd%d" % b)
+            inc(v.tensor_scalar(T.bc[0:k, 128 * b:128 * b + 128], T.pm[0:k, :], col, None, ADD), "bcd%d" % b)
+            if b < NB - 1:
+                wait("y", "cb%d" % b)
+                q = 8 * sources(rank, b)[0]
+                inc(sy.dma_start(T.nb[0:1, q:q + k, 0], col), "nd", 16)
         else:
-            inc(v.tensor_scalar(T.bc[0:16, 128 * b:128 * b + 128], T.pm[0:16, :], 4.0, col, AluOpType.mult, ADD), "bcd%d" % b)
+            inc(v.tensor_scalar(T.bc[0:k, 128 * b:128 * b + 128], T.pm[0:k, :], 4.0, col, AluOpType.mult, ADD), "bcd%d" % b)
         wait("t", "bcd%d" % b)
         if b:
             wait("t", "ofd%d" % (b - 1))
         inc(pe.transpose(T.ob[:, 0:128], T.bc[:, 128 * b:128 * b + 128], T.ident[:, :]), "obd%d" % b)
-        wait("v", "obd%d" % b)
 
-    goals = c_targets(rank)
-    for b in range(NB):
-        src = groups[(m - step[b]) % ng]
-        for r in src:
-            expect("w%d" % r, 2 * n_off)
-            wait("t", "w%d" % r)
-        c0 = Q * src[0]
-        for h, bank in enumerate((T.sc0, T.sc1)):
-            if b:
-                wait("t", ("saa%d", "sab%d")[h] % (b - 1))
-            inc(pe.matmul_mx(bank[:, 0:256], T.xq[:, 128 * h:128 * h + 128], T.xs[:, 128 * h:128 * h + 128],
-                             T.wq[:, c0:c0 + 256], T.ws[:, c0:c0 + 256], True, True), ("mma%d", "mmb%d")[h] % b)
-        wait("v", "ms")
-        for h, bank in enumerate((T.sc0, T.sc1)):
-            wait("v", ("mma%d", "mmb%d")[h] % b)
-            inc(v.tensor_tensor_scan(T.S[:, 512 * b + 256 * h:512 * b + 256 * h + 256], T.rst[:, :], bank[:, 0:256], 0.0, ADD, MAX),
-                ("saa%d", "sab%d")[h] % b)
-        choose(b)
-        for u in range(4):
-            inc(v.tensor_scalar(T.of[:, 64 * b + u:64 * b + 64:4], T.ob[:, 0:16], float(16 * u), None, ADD), "ofd%d" % b)
+    def offsets(b):
+        k = 8 * width(b)
+        wait("v", "obd%d" % b)
+        if b < NB:
+            for u in range(4):
+                inc(v.tensor_scalar(T.of[:, 64 * b + u:64 * b + 4 * k:4], T.ob[:, 0:k], float(16 * u), None, ADD), "ofd%d" % b)
+        else:
+            inc(v.tensor_scalar(T.of[:, 64 * b:64 * b + k], T.ob[:, 0:k], 0.25, None, AluOpType.mult), "ofd%d" % b)
         wait("v", "ofd%d" % b)
+
+    def gather_x(b, j, q, a, e):
+        i, f = 2 * b + j, 64 * b + 32 * j
+        out, win = T.gt[:, 1024 * i + a:1024 * i + e], T.xr[:, 0:1024].indirect(T.of[:, f + a // 16:f + e // 16])
+        wait(q, "ofd%d" % b)
+        inc(v.tensor_copy(out, win) if q == "v" else act.activation(out, win, COPY), "gx%d" % i if q == "v" else "gr%d" % i)
+
+    def gather_r(b, j):
+        i, f = 2 * b + j, 64 * b + 32 * j
         wait("s", "ofd%d" % b)
         wait("s", "rs")
-        for j, (r, rel) in enumerate(goals[b]):
-            i = 2 * b + j
-            f0 = 64 * b + 32 * src.index(r)
-            inc(v.tensor_copy(T.gt[:, 1024 * i:1024 * i + 512], T.xr[:, 0:1024].indirect(T.of[:, f0:f0 + 32])), "gx%d" % i)
-            inc(act.activation(T.gt[:, 1024 * i + 512:1024 * i + 1024], T.xr[:, 1024:2048].indirect(T.of[:, f0:f0 + 32]), COPY), "gr%d" % i)
-            wait("v", "gx%d" % i)
-            wait("v", "gr%d" % i)
-            inc(v.quantize_mx(T.cq[:, 256 * i:256 * i + 256], T.cs[:, 256 * i:256 * i + 256], T.gt[:, 1024 * i:1024 * i + 1024]), "qz%d" % i)
-        wait("y", "cb%d" % b)
-        inc(sy.dma_start(T.nb[0:1, 8 * src[0]:8 * src[0] + 16, 0], T.cc[0:16, 4 * b:4 * b + 1]), "nd", 16)
-        for j, (r, rel) in enumerate(goals[b]):
-            i = 2 * b + j
-            wait("g", "qz%d" % i)
-            if rel:
-                send([helper], T.cq[:, 256 * i:256 * i + 256].bitcast(dt.uint8), T.cq[:, 256 * i:256 * i + 256].bitcast(dt.uint8), "hc%d" % i)
-                send([helper], T.cs[:, 256 * i:256 * i + 256], T.cs[:, 256 * i:256 * i + 256], "hc%d" % i)
-            else:
-                send_c(cores[r], i, rank)
-            if b == NB - 1 and j == 0:
-                wait("g", "nd")
-                others = [cores[o] for k in range(ng) if k != m for o in groups[k]]
-                send(others, T.nb[0], T.nl[rank], "nm", 1 << offe[-1])
+        inc(act.activation(T.gt[:, 1024 * i + 512:1024 * i + 1024], T.xr[:, 1024:2048].indirect(T.of[:, f:f + 32]), COPY), "gr%d" % i)
 
-    own = {rank: (T.xq, T.xs), mate: (T.pq, T.ps)}
-    wcols = T.wq[:, Q * rank:Q * rank + Q], T.ws[:, Q * rank:Q * rank + Q]
-    expect("pa", 2 * n_on)
+    def pack(b, j):
+        i = 2 * b + j
+        wait("v", "gx%d" % i)
+        wait("v", "gr%d" % i)
+        inc(v.quantize_mx(T.cq[:, 256 * i:256 * i + 256], T.cs[:, 256 * i:256 * i + 256], T.gt[:, 1024 * i:1024 * i + 1024]), "qz%d" % i)
+
+    def ship(b, j):
+        i, d = 2 * b + j, cores[sources(rank, b)[j]]
+        wait("g", "qz%d" % i)
+        if c_relay(b):
+            send([helper], T.cq[:, 256 * i:256 * i + 256].bitcast(dt.uint8), T.cq[:, 256 * i:256 * i + 256].bitcast(dt.uint8), "hc%d" % i)
+            send([helper], T.cs[:, 256 * i:256 * i + 256], T.cs[:, 256 * i:256 * i + 256], "hc%d" % i)
+        else:
+            send_c(d, i, rank)
+
+    products(0)
+    over_queries(0)
+    over_items(0)
+    offsets(0)
+    for b in range(NB):
+        last = b == NB - 1
+        items = range(width(b))
+        for j in items:
+            gather_r(b, j)
+        if not last:
+            gather_x(b, 1, "s", 256, 512)
+        gather_x(b, 0, "v", 0, 512)
+        pack(b, 0)
+        if not last:
+            products(b + 1)
+            over_queries(b + 1)
+            gather_x(b, 1, "v", 0, 256)
+            pack(b, 1)
+            over_items(b + 1)
+            offsets(b + 1)
+        for j in items:
+            ship(b, j)
+        if b == NB - 2:
+            wait("g", "nd")
+            send([cores[o] for k in range(NB - 1) for o in sources(rank, k)], T.nb[0], T.nl[rank], "nm", 1 << offe[-1])
+            wait("g", "cb%d" % (NB - 1))
+            send([cores[sources(rank, NB - 1)[0]]], T.cc[:, 4 * NB - 4:4 * NB - 3], T.nx[:, :], "nx")
+
     b = NB
-    banks = {rank: (T.sc0, T.sc1), mate: (T.y0, T.y1)}
-    wait("t", "rs")
-    wait("t", "wqd")
-    wait("t", "rq")
-    for s in (rank, mate):
-        if s == mate:
-            wait("t", "pa")
-        for h in range(2):
-            if s == rank:
-                wait("t", ("saa%d", "sab%d")[h] % (b - 1))
-            inc(pe.matmul_mx(banks[s][h][:, 0:128], own[s][0][:, 128 * h:128 * h + 128], own[s][1][:, 128 * h:128 * h + 128],
-                             wcols[0], wcols[1], True, True), ("mma%d", "mmb%d")[h] % b)
-    for l, s in enumerate(duo):
-        bank = (T.y2, T.y3)[l]
-        pe.matmul_mx(bank[:, 0:IT], wcols[0], wcols[1], own[s][0][:, 0:IT], own[s][1][:, 0:IT], True, False)
-        inc(pe.matmul_mx(bank[:, 0:IT], wcols[0], wcols[1], own[s][0][:, IT:2 * IT], own[s][1][:, IT:2 * IT], False, True), "fa%d" % l)
-    for h in range(2):
-        wait("v", ("mma%d", "mmb%d")[h] % b)
-        for l, s in enumerate(duo):
-            o = 512 * b + 256 * h + 128 * l
-            inc(v.tensor_tensor_scan(T.S[:, o:o + 128], T.rst[:, 0:128], banks[s][h][:, 0:128], 0.0, ADD, MAX), ("saa%d", "sab%d")[h] % b)
-    for l in range(2):
+    products(b)
+    over_queries(b)
+    wide = (T.sc0, T.sc1, T.y0)
+    for l, s in enumerate(near):
+        wait("t", ("saa%d" if l != 1 else "sab%d") % b)
+        pe.matmul_mx(wide[l][:, 0:IT], wcols[0], wcols[1], own[s][0][:, 0:IT], own[s][1][:, 0:IT], True, False)
+        inc(pe.matmul_mx(wide[l][:, 0:IT], wcols[0], wcols[1], own[s][0][:, IT:2 * IT], own[s][1][:, IT:2 * IT], False, True), "fa%d" % l)
         wait("s", "fa%d" % l)
-        inc(act.activation(T.ab[:, IT * l:IT * l + IT], (T.y2, T.y3)[l][:, 0:IT], COPY), "fb")
-    choose(b)
-    inc(v.tensor_scalar(T.of[:, 64 * b:64 * b + 16], T.ob[:, 0:16], 0.25, None, AluOpType.mult), "ofd%d" % b)
-    wait("v", "ofd%d" % b)
-    wait("v", "fb")
-    for l, s in enumerate(duo):
-        f0 = 64 * b + 8 * l
-        inc(v.tensor_copy(T.yt[:, 128 * s:128 * s + 128], T.ab[:, IT * l:IT * l + IT].indirect(T.of[:, f0:f0 + 8])), "fg")
+        inc(act.activation(T.ab[:, IT * l:IT * l + IT], wide[l][:, 0:IT], COPY), "fb")
+    over_items(b)
     wait("y", "cb%d" % b)
     inc(sy.dma_start(T.cht[duo[0]:duo[0] + 2, 0:8], T.cc[0:16, 4 * b:4 * b + 1]), "ct", 16)
-    wait("y", "fg")
-    inc(sy.dma_start(T.y[:, 128 * duo[0]:128 * duo[0] + 256], T.yt[:, 128 * duo[0]:128 * duo[0] + 256]), "sf", 16)
+    inc(sy.dma_start(T.cht[peer:peer + 1, 0:8], T.cc[16:24, 4 * b:4 * b + 1]), "ct", 16)
+    offsets(b)
+    wait("v", "fb")
+    for l, s in enumerate(near):
+        f0 = 64 * b + 8 * l
+        inc(v.tensor_copy(T.yt[:, 128 * s:128 * s + 128], T.ab[:, IT * l:IT * l + IT].indirect(T.of[:, f0:f0 + 8])), "fg")
+    wait("s", "fg")
+    inc(act.dma_start(T.y[:, 128 * duo[0]:128 * duo[0] + 256], T.yt[:, 128 * duo[0]:128 * duo[0] + 256]), "sy", 16)
+    inc(act.dma_start(T.y[:, 128 * peer:128 * peer + 128], T.yt[:, 128 * peer:128 * peer + 128]), "sy", 16)
 
-    freed = ["saa%d" % NB, "sab%d" % NB, "fb", "fb"]
-    for b in range(NB):
-        for j, s in enumerate(groups[(m + step[b]) % ng]):
+    order = [(T.y3, "sab%d" % NB), (T.y0, "fb"), (T.y1, "sab%d" % NB), (T.y2, "saa%d" % NB), (T.y1, "fy2")]
+    for b in (1, 0, 2):
+        for j, s in enumerate(owners(rank, b)):
             i = 2 * b + j
-            bank = ybank[i % 4]
+            bank, free = order[i]
             expect("c%d" % s, 2 * n_off)
-            wait("t", freed[i] if i < 4 else "fy%d" % (i - 4))
+            wait("t", free)
             wait("t", "c%d" % s)
             pe.matmul_mx(bank[:, 0:128], wcols[0], wcols[1], T.lq[:, 256 * s:256 * s + 128], T.ls[:, 256 * s:256 * s + 128], True, False)
             inc(pe.matmul_mx(bank[:, 0:128], wcols[0], wcols[1], T.lq[:, 256 * s + 128:256 * s + 256],
@@ -371,16 +426,20 @@ def rank_program(g, core, T, topo):
             wait("s", "fy%d" % i)
             inc(act.dma_start(T.y[:, 128 * s:128 * s + 128], T.yt[:, 128 * s:128 * s + 128]), "sy", 16)
 
-    expect("nm", len(cores) - len(duo))
+    expect("nm", sum(len(owners(rank, k)) for k in range(NB - 1)))
+    expect("nx", n_off)
     wait("y", "nm")
-    for k in range(ng):
-        if k != m:
-            s = groups[k][0]
-            inc(sy.dma_start(T.cht[s:s + 2, 0:8], T.nl[s:s + 2, 8 * rank:8 * rank + 8, 0]), "ct", 16)
+    for k in range(NB - 1):
+        s = owners(rank, k)[0]
+        inc(sy.dma_start(T.cht[s:s + 2, 0:8], T.nl[s:s + 2, 8 * rank:8 * rank + 8, 0]), "ct", 16)
     wait("v", "ct")
     inc(v.transpose(T.chu[:, :], T.cht[:, :]), "ch1")
     wait("v", "ch1")
     inc(v.tensor_scalar(T.cho[0:8, 0:8], T.chu[0:8, 0:8], 1.0 / 64.0, None, AluOpType.mult), "ch2")
-    wait("y", "ch2")
+    wait("v", "ch2")
+    wait("v", "nx")
+    s = owners(rank, NB - 1)[0]
+    inc(v.tensor_scalar(T.cho[0:8, s:s + 1], T.nx[0:8, :], 1.0 / 64.0, None, AluOpType.mult), "ch3")
+    wait("y", "ch3")
     inc(sy.dma_start(T.ch[:, :], T.cho[0:8, 0:8]), "sc", 16)
     finish()

@@ -56,20 +56,12 @@ SCRATCH = {
 }
 SEMAPHORES = (
     ["ldq", "ldx", "kone", "ms", "mz", "kz", "kid", "kpm", "eqd", "wqd", "xqd", "rs", "rq", "lsem", "pa", "pf", "nm", "nx",
-     "nz", "nd", "ct", "sc", "sy", "hw", "fa0", "fa1", "fa2", "fb", "fg", "ch1", "ch2", "ch3"]
+     "nz", "nd", "ct", "sc", "sy", "fa0", "fa1", "fa2", "fb", "fg", "ch1", "ch2", "ch3"]
     + ["dm%d" % b for b in range(4)]
     + ["%s%d" % (k, b) for b in range(4) for k in ("mma", "mmb", "saa", "sab", "trd", "s2", "ltd", "cb", "bcd", "obd", "ofd")]
     + ["%s%d" % (k, i) for i in range(NI) for k in ("gx", "gr", "qz", "fm", "fy")]
     + ["w%d" % r for r in range(NR)] + ["c%d" % r for r in range(NR)] + ["hc%d" % i for i in range(NI)]
 )
-
-
-def w_relay(b, same):
-    return b == 1 and not same
-
-
-def c_relay(b):
-    return b == 0
 
 
 def rank_program(g, core, T, topo):
@@ -88,18 +80,21 @@ def rank_program(g, core, T, topo):
             place[groups[k][j]] = (k, j)
     step = sorted(range(1, ng), key=lambda d: topo.same_plane(chips[0], chips[d]))
 
+    def same(r, s):
+        return place[r][1] == place[s][1]
+
     def peer_of(r):
         k, j = place[r]
         return groups[(k + step[-1]) % ng][j]
 
     def sources(r, b):
-        return [s for s in groups[(place[r][0] - step[b]) % ng] if s != peer_of(r)]
+        return sorted([s for s in groups[(place[r][0] - step[b]) % ng] if s != peer_of(r)], key=lambda s: same(r, s))
 
     def owners(r, b):
         return [s for s in groups[(place[r][0] + step[b]) % ng] if s != peer_of(r)]
 
-    def w_roads(r, relay):
-        return [[s for s in owners(r, b) if w_relay(b, place[s][1] == place[r][1]) == relay] for b in range(NB)]
+    def relayed(b, r, s):
+        return b < NB - 1 and not same(r, s)
 
     def helper_of(r):
         own = cores[r]
@@ -155,11 +150,6 @@ def rank_program(g, core, T, topo):
     n_off, n_on = len(offe), len([e for e in topo.engines(core, [c for c in topo.cores_of(core) if c != core][0])
                                   if e not in offe])
 
-    def send_w(dsts, r, sem):
-        codes, plane = T.wq[:, Q * r:Q * r + Q].bitcast(dt.uint8), T.ws[:, Q * r:Q * r + Q]
-        send(dsts, codes, codes, sem)
-        send(dsts, plane, plane, sem)
-
     def send_xr(dst, codes, plane, codes2, plane2, sem):
         send([dst], codes[:, :].bitcast(dt.uint8), codes2[:, :].bitcast(dt.uint8), sem)
         send([dst], plane[:, :], plane2[:, :], sem)
@@ -172,17 +162,12 @@ def rank_program(g, core, T, topo):
     if rank is None:
         for r in range(len(cores)):
             if helper_of(r) == core:
-                expect("hw", 2 * n_on)
-                wait("g", "hw")
-                for l in w_roads(r, True):
-                    if l:
-                        send_w([cores[s] for s in l], r, "w%d" % r)
                 expect("pa", 2 * n_on)
                 wait("g", "pa")
                 send_xr(cores[peer_of(r)], T.pq, T.ps, T.fq, T.fs, "pf")
                 for b in range(NB):
                     for j, d in enumerate(sources(r, b)):
-                        if c_relay(b):
+                        if relayed(b, d, r):
                             i = 2 * b + j
                             expect("hc%d" % i, 2 * n_on)
                             wait("g", "hc%d" % i)
@@ -221,10 +206,10 @@ def rank_program(g, core, T, topo):
     wcols = T.wq[:, w0:w0 + Q], T.ws[:, w0:w0 + Q]
     inc(v.quantize_mx(wcols[0], wcols[1], T.qt[:, :]), "wqd")
     wait("g", "wqd")
-    for b, l in enumerate(w_roads(rank, False)):
-        send_w([cores[s] for s in l], rank, "w%d" % rank)
-        if b == 0:
-            send_w([helper], rank, "hw")
+    for b in range(NB):
+        to = [cores[s] for s in owners(rank, b)]
+        send(to, wcols[0].bitcast(dt.uint8), wcols[0].bitcast(dt.uint8), "w%d" % rank)
+        send(to, wcols[1], wcols[1], "w%d" % rank)
 
     wait("v", "ldx")
     inc(v.quantize_mx(T.xq[:, 0:IT], T.xs[:, 0:IT], T.xr[:, 0:4 * IT]), "xqd")
@@ -263,7 +248,7 @@ def rank_program(g, core, T, topo):
             for r in src:
                 expect("w%d" % r, 2 * n_off)
                 wait("t", "w%d" % r)
-            c0, n = Q * src[0], Q * len(src)
+            c0, n = Q * min(src), Q * len(src)
             for h in range(2):
                 if b:
                     wait("t", ("saa%d", "sab%d")[h] % (b - 1))
@@ -313,7 +298,7 @@ def rank_program(g, core, T, topo):
             inc(v.tensor_scalar(T.bc[0:k, 128 * b:128 * b + 128], T.pm[0:k, :], col, None, ADD), "bcd%d" % b)
             if b < NB - 1:
                 wait("y", "cb%d" % b)
-                q = 8 * sources(rank, b)[0]
+                q = 8 * min(sources(rank, b))
                 inc(sy.dma_start(T.nb[0:1, q:q + k, 0], col), "nd", 16)
         else:
             inc(v.tensor_scalar(T.bc[0:k, 128 * b:128 * b + 128], T.pm[0:k, :], 4.0, col, AluOpType.mult, ADD), "bcd%d" % b)
@@ -332,14 +317,18 @@ def rank_program(g, core, T, topo):
             inc(v.tensor_scalar(T.of[:, 64 * b:64 * b + k], T.ob[:, 0:k], 0.25, None, AluOpType.mult), "ofd%d" % b)
         wait("v", "ofd%d" % b)
 
+    def lists(b, j):
+        src = sources(rank, b)
+        return 64 * b + 32 * sorted(src).index(src[j])
+
     def gather_x(b, j, q, a, e):
-        i, f = 2 * b + j, 64 * b + 32 * j
+        i, f = 2 * b + j, lists(b, j)
         out, win = T.gt[:, 1024 * i + a:1024 * i + e], T.xr[:, 0:1024].indirect(T.of[:, f + a // 16:f + e // 16])
         wait(q, "ofd%d" % b)
         inc(v.tensor_copy(out, win) if q == "v" else act.activation(out, win, COPY), "gx%d" % i if q == "v" else "gr%d" % i)
 
     def gather_r(b, j):
-        i, f = 2 * b + j, 64 * b + 32 * j
+        i, f = 2 * b + j, lists(b, j)
         wait("s", "ofd%d" % b)
         wait("s", "rs")
         inc(act.activation(T.gt[:, 1024 * i + 512:1024 * i + 1024], T.xr[:, 1024:2048].indirect(T.of[:, f:f + 32]), COPY), "gr%d" % i)
@@ -351,13 +340,13 @@ def rank_program(g, core, T, topo):
         inc(v.quantize_mx(T.cq[:, 256 * i:256 * i + 256], T.cs[:, 256 * i:256 * i + 256], T.gt[:, 1024 * i:1024 * i + 1024]), "qz%d" % i)
 
     def ship(b, j):
-        i, d = 2 * b + j, cores[sources(rank, b)[j]]
+        i, d = 2 * b + j, sources(rank, b)[j]
         wait("g", "qz%d" % i)
-        if c_relay(b):
+        if relayed(b, d, rank):
             send([helper], T.cq[:, 256 * i:256 * i + 256].bitcast(dt.uint8), T.cq[:, 256 * i:256 * i + 256].bitcast(dt.uint8), "hc%d" % i)
             send([helper], T.cs[:, 256 * i:256 * i + 256], T.cs[:, 256 * i:256 * i + 256], "hc%d" % i)
         else:
-            send_c(d, i, rank)
+            send_c(cores[d], i, rank)
 
     products(0)
     over_queries(0)
@@ -371,10 +360,11 @@ def rank_program(g, core, T, topo):
         if not last:
             gather_x(b, 1, "s", 256, 512)
         gather_x(b, 0, "v", 0, 512)
-        pack(b, 0)
         if not last:
             products(b + 1)
             over_queries(b + 1)
+        pack(b, 0)
+        if not last:
             gather_x(b, 1, "v", 0, 256)
             pack(b, 1)
             over_items(b + 1)
@@ -387,6 +377,25 @@ def rank_program(g, core, T, topo):
             wait("g", "cb%d" % (NB - 1))
             send([cores[sources(rank, NB - 1)[0]]], T.cc[:, 4 * NB - 4:4 * NB - 3], T.nx[:, :], "nx")
 
+    order = [(T.y1, "sab%d" % NB), (T.y2, "saa%d" % NB), (T.y3, "sab%d" % NB), (T.y0, "fb")]
+    tiles = [(b, s) for b in range(NB) for s in owners(rank, b)]
+    tiles.sort(key=lambda e: (2 + 2 * e[0]) if relayed(e[0], e[1], rank) else (0, 1, 3)[e[0]])
+
+    def final(l):
+        for p in l:
+            s = tiles[p][1]
+            bank = order[p % 4][0]
+            expect("c%d" % s, 2 * n_off)
+            wait("t", order[p][1] if p < 4 else "fy%d" % (p - 4))
+            wait("t", "c%d" % s)
+            pe.matmul_mx(bank[:, 0:128], wcols[0], wcols[1], T.lq[:, 256 * s:256 * s + 128], T.ls[:, 256 * s:256 * s + 128], True, False)
+            inc(pe.matmul_mx(bank[:, 0:128], wcols[0], wcols[1], T.lq[:, 256 * s + 128:256 * s + 256],
+                             T.ls[:, 256 * s + 128:256 * s + 256], False, True), "fm%d" % p)
+            wait("s", "fm%d" % p)
+            inc(act.activation(T.yt[:, 128 * s:128 * s + 128], bank[:, 0:128], COPY), "fy%d" % p)
+            wait("s", "fy%d" % p)
+            inc(act.dma_start(T.y[:, 128 * s:128 * s + 128], T.yt[:, 128 * s:128 * s + 128]), "sy", 16)
+
     b = NB
     products(b)
     over_queries(b)
@@ -397,6 +406,7 @@ def rank_program(g, core, T, topo):
         inc(pe.matmul_mx(wide[l][:, 0:IT], wcols[0], wcols[1], own[s][0][:, IT:2 * IT], own[s][1][:, IT:2 * IT], False, True), "fa%d" % l)
         wait("s", "fa%d" % l)
         inc(act.activation(T.ab[:, IT * l:IT * l + IT], wide[l][:, 0:IT], COPY), "fb")
+    final(range(0, 2))
     over_items(b)
     wait("y", "cb%d" % b)
     inc(sy.dma_start(T.cht[duo[0]:duo[0] + 2, 0:8], T.cc[0:16, 4 * b:4 * b + 1]), "ct", 16)
@@ -409,22 +419,7 @@ def rank_program(g, core, T, topo):
     wait("s", "fg")
     inc(act.dma_start(T.y[:, 128 * duo[0]:128 * duo[0] + 256], T.yt[:, 128 * duo[0]:128 * duo[0] + 256]), "sy", 16)
     inc(act.dma_start(T.y[:, 128 * peer:128 * peer + 128], T.yt[:, 128 * peer:128 * peer + 128]), "sy", 16)
-
-    order = [(T.y3, "sab%d" % NB), (T.y0, "fb"), (T.y1, "sab%d" % NB), (T.y2, "saa%d" % NB), (T.y1, "fy2")]
-    for b in (1, 0, 2):
-        for j, s in enumerate(owners(rank, b)):
-            i = 2 * b + j
-            bank, free = order[i]
-            expect("c%d" % s, 2 * n_off)
-            wait("t", free)
-            wait("t", "c%d" % s)
-            pe.matmul_mx(bank[:, 0:128], wcols[0], wcols[1], T.lq[:, 256 * s:256 * s + 128], T.ls[:, 256 * s:256 * s + 128], True, False)
-            inc(pe.matmul_mx(bank[:, 0:128], wcols[0], wcols[1], T.lq[:, 256 * s + 128:256 * s + 256],
-                             T.ls[:, 256 * s + 128:256 * s + 256], False, True), "fm%d" % i)
-            wait("s", "fm%d" % i)
-            inc(act.activation(T.yt[:, 128 * s:128 * s + 128], bank[:, 0:128], COPY), "fy%d" % i)
-            wait("s", "fy%d" % i)
-            inc(act.dma_start(T.y[:, 128 * s:128 * s + 128], T.yt[:, 128 * s:128 * s + 128]), "sy", 16)
+    final(range(2, NI))
 
     expect("nm", sum(len(owners(rank, k)) for k in range(NB - 1)))
     expect("nx", n_off)

from concourse.bass import DstId, RemoteDMATransfer
from concourse.mybir import dt, AluOpType, ActivationFunctionType, AxisListType

NR, Q, IT = 8, 128, 256
LOW = -5.0e29
NB = 3
NI = 5

SCRATCH = {
    "qt": ("sbuf", [128, 4 * Q], "bfloat16"),
    "xr": ("sbuf", [128, 8 * IT], "bfloat16"),
    "onb": ("sbuf", [128, 516], "bfloat16"),
    "onf": ("sbuf", [128, 128], "float32"),
    "zt": ("sbuf", [128, 516], "bfloat16"),
    "ident": ("sbuf", [128, 128], "float32"),
    "pm": ("sbuf", [128, 128], "float32"),
    "rst": ("sbuf", [128, 256], "float32"),
    "neg": ("sbuf", [128, 256], "float32"),
    "eq": ("sbuf", [128, 512], "float8_e4m3fn_x4"),
    "es": ("sbuf", [128, 512], "uint8"),
    "wq": ("sbuf", [128, NR * Q], "float8_e4m3fn_x4"),
    "ws": ("sbuf", [128, NR * Q], "uint8"),
    "xq": ("sbuf", [128, 2 * IT], "float8_e4m3fn_x4"),
    "xs": ("sbuf", [128, 2 * IT], "uint8"),
    "pq": ("sbuf", [128, 2 * IT], "float8_e4m3fn_x4"),
    "ps": ("sbuf", [128, 2 * IT], "uint8"),
    "fq": ("sbuf", [128, 2 * IT], "float8_e4m3fn_x4"),
    "fs": ("sbuf", [128, 2 * IT], "uint8"),
    "S": ("sbuf", [128, 2304], "float32"),
    "P": ("sbuf", [128, 1024], "float32"),
    "lt": ("sbuf", [128, 64], "float32"),
    "cc": ("sbuf", [128, 16], "float32"),
    "bc": ("sbuf", [128, 512], "float32"),
    "of": ("sbuf", [128, 256], "uint16"),
    "gt": ("sbuf", [128, NI * 1024], "bfloat16"),
    "cq": ("sbuf", [128, NI * 256], "float8_e4m3fn_x4"),
    "cs": ("sbuf", [128, NI * 256], "uint8"),
    "lq": ("sbuf", [128, NR * 256], "float8_e4m3fn_x4"),
    "ls": ("sbuf", [128, NR * 256], "uint8"),
    "ab": ("sbuf", [128, 3 * IT], "float32"),
    "yt": ("sbuf", [128, 1024], "float32"),
    "cht": ("sbuf", [32, 32], "float32"),
    "chu": ("sbuf", [32, 32], "float32"),
    "cho": ("sbuf", [32, 8], "float32"),
    "nx": ("sbuf", [128, 1], "float32"),
    "nb": ("dram", [1, 128, 1], "float32"),
    "nl": ("dram", [NR, 128, 1], "float32"),
    "sc0": ("psum", [128, 512], "float32"),
    "sc1": ("psum", [128, 512], "float32"),
    "tr": ("psum", [128, 512], "float32"),
    "ob": ("psum", [128, 512], "float32"),
    "y0": ("psum", [128, 512], "float32"),
    "y1": ("psum", [128, 512], "float32"),
    "y2": ("psum", [128, 512], "float32"),
    "y3": ("psum", [128, 512], "float32"),
}
SEMAPHORES = (
    ["ldq", "ldx", "kone", "ms", "mz", "kz", "kid", "kpm", "eqd", "wqd", "xqd", "rs", "rq", "lsem", "pa", "pf", "nm", "nx",
     "nz", "nd", "ct", "sc", "sy", "fa0", "fa1", "fa2", "fb", "fg", "ch1", "ch2", "ch3"]
    + ["dm%d" % b for b in range(4)]
    + ["%s%d" % (k, b) for b in range(4) for k in ("mma", "mmb", "saa", "sab", "trd", "s2", "ltd", "cb", "bcd", "obd", "ofd")]
    + ["%s%d" % (k, i) for i in range(NI) for k in ("gx", "gr", "qz", "fm", "fy")]
    + ["w%d" % r for r in range(NR)] + ["c%d" % r for r in range(NR)] + ["hc%d" % i for i in range(NI)]
)


def rank_program(g, core, T, topo):
    cores = list(T.cores)
    groups, chips = [], []
    for r in range(len(cores)):
        c = topo.chip(cores[r])
        if c not in chips:
            chips.append(c)
            groups.append([])
        groups[chips.index(c)].append(r)
    ng = len(groups)
    place = {}
    for k in range(ng):
        for j in range(len(groups[k])):
            place[groups[k][j]] = (k, j)
    step = sorted(range(1, ng), key=lambda d: topo.same_plane(chips[0], chips[d]))

    def same(r, s):
        return place[r][1] == place[s][1]

    def peer_of(r):
        k, j = place[r]
        return groups[(k + step[-1]) % ng][j]

    def sources(r, b):
        return sorted([s for s in groups[(place[r][0] - step[b]) % ng] if s != peer_of(r)], key=lambda s: same(r, s))

    def owners(r, b):
        return [s for s in groups[(place[r][0] + step[b]) % ng] if s != peer_of(r)]

    def relayed(b, r, s):
        return b < NB - 1 and not same(r, s)

    def helper_of(r):
        own = cores[r]
        far = [c for c in topo.cores_of(own) if topo.die(c) != topo.die(own) and T.rank_of(c) is None
               and all(topo.may_write(c, t) for t in cores)]
        return far[place[r][1]]

    queue = {"g": g, "v": g.vector, "s": g.scalar, "t": g.tensor, "y": g.sync}
    cnt, seen, top = {}, {}, {}

    def inc(ins, name, k=1):
        ins.then_inc(T.sem[name], k)
        cnt[name] = cnt.get(name, 0) + k

    def wait(q, name):
        v = cnt[name]
        if seen.get((q, name), 0) < v:
            queue[q].wait_ge(T.sem[name], v)
            seen[(q, name)] = v
            top[name] = max(top.get(name, 0), v)

    def expect(name, k):
        cnt[name] = cnt.get(name, 0) + k

    def finish():
        for name in cnt:
            if top.get(name, 0) < cnt[name]:
                wait("g", name)

    far_core = [c for c in cores if topo.chip(c) != topo.chip(core)][0]
    offe = topo.engines(core, far_core)

    def mask_to(dst):
        if topo.chip(dst) != topo.chip(core):
            return topo.mask(core, dst)
        return sum(1 << e for e in topo.engines(core, dst) if e not in offe)

    def send(dsts, src, dst, sem, mask=None):
        m = mask_to(dsts[0]) if mask is None else mask
        if len(dsts) == 1:
            rid, pid, _ = topo.addr(dsts[0])
            g.remote_dma(out_ap=dst, in_ap=src, remote_sem=T.sem[sem], local_sem=T.sem["lsem"], pid=pid,
                         routing_id=rid, dma_engine_mask=m)
        else:
            ids = []
            for d in dsts:
                rid, pid, _ = topo.addr(d)
                ids.append(DstId(rid=rid, pnc=pid))
            g.remote_dma_fused([RemoteDMATransfer(dst_ids=ids, dma_engine_mask=m, remote_sem=T.sem[sem], srcs=[src],
                                                  dsts=[dst] * len(dsts))], local_sem=T.sem["lsem"])
        cnt["lsem"] = cnt.get("lsem", 0) + bin(m).count("1")

    n_off, n_on = len(offe), len([e for e in topo.engines(core, [c for c in topo.cores_of(core) if c != core][0])
                                  if e not in offe])

    def send_xr(dst, codes, plane, codes2, plane2, sem):
        send([dst], codes[:, :].bitcast(dt.uint8), codes2[:, :].bitcast(dt.uint8), sem)
        send([dst], plane[:, :], plane2[:, :], sem)

    def send_c(dst, i, s):
        send([dst], T.cq[:, 256 * i:256 * i + 256].bitcast(dt.uint8), T.lq[:, 256 * s:256 * s + 256].bitcast(dt.uint8), "c%d" % s)
        send([dst], T.cs[:, 256 * i:256 * i + 256], T.ls[:, 256 * s:256 * s + 256], "c%d" % s)

    rank = T.rank_of(core)
    if rank is None:
        for r in range(len(cores)):
            if helper_of(r) == core:
                expect("pa", 2 * n_on)
                wait("g", "pa")
                send_xr(cores[peer_of(r)], T.pq, T.ps, T.fq, T.fs, "pf")
                for b in range(NB):
                    for j, d in enumerate(sources(r, b)):
                        if relayed(b, d, r):
                            i = 2 * b + j
                            expect("hc%d" % i, 2 * n_on)
                            wait("g", "hc%d" % i)
                            send_c(cores[d], i, r)
                finish()
        return

    m, _ = place[rank]
    duo = groups[m]
    mate = [r for r in duo if r != rank][0]
    peer = peer_of(rank)
    near = duo + [peer]
    helper = helper_of(rank)
    v, pe, act, sy = g.vector, g.tensor, g.scalar, g.sync
    COPY = ActivationFunctionType.Copy
    ADD, MAX = AluOpType.add, AluOpType.max

    inc(sy.dma_start(T.qt[:, :], T.qw[:, :]), "ldq", 16)
    inc(sy.dma_start(T.xr[:, 0:4 * IT], T.x[:, :]), "ldx", 16)

    inc(v.memset(T.onb[:, :], 1.0), "kone")
    inc(v.memset(T.onf[:, :], 1.0), "kone")
    inc(v.memset(T.rst[:, :], 0.0), "mz")
    inc(v.memset(T.bc[:, :], 0.0), "ms")
    inc(v.memset(T.neg[:, :], LOW), "ms")
    inc(v.memset(T.cht[:, :], 0.0), "ms")
    inc(v.memset(T.cc[:, :], 0.0), "ms")
    wait("v", "mz")
    inc(v.memset(T.rst[:, 0:256:16], LOW), "ms")
    wait("g", "kone")
    inc(g.affine_select(T.zt[:, :], T.onb[:, :], [[-1, 516]], AluOpType.is_equal, 0.0, 3, 4), "kz")
    inc(g.affine_select(T.ident[:, :], T.onf[:, :], [[-1, 128]], AluOpType.is_equal, 0.0, 0, 1), "kid")

    wait("v", "ldq")
    w0 = Q * rank
    wcols = T.wq[:, w0:w0 + Q], T.ws[:, w0:w0 + Q]
    inc(v.quantize_mx(wcols[0], wcols[1], T.qt[:, :]), "wqd")
    wait("g", "wqd")
    for b in range(NB):
        to = [cores[s] for s in owners(rank, b)]
        send(to, wcols[0].bitcast(dt.uint8), wcols[0].bitcast(dt.uint8), "w%d" % rank)
        send(to, wcols[1], wcols[1], "w%d" % rank)

    wait("v", "ldx")
    inc(v.quantize_mx(T.xq[:, 0:IT], T.xs[:, 0:IT], T.xr[:, 0:4 * IT]), "xqd")
    wait("v", "kz")
    for b in range(4):
        inc(v.quantize_mx(T.eq[:, 128 * b:128 * b + 128], T.es[:, 128 * b:128 * b + 128], T.zt[:, 3 - b:3 - b + 512]), "eqd")
    wait("t", "xqd")
    wait("t", "eqd")
    ybank = [T.y0, T.y1, T.y2, T.y3]
    for b in range(4):
        inc(pe.matmul_mx(ybank[b][:, 0:IT], T.eq[:, 128 * b:128 * b + 128], T.es[:, 128 * b:128 * b + 128],
                         T.xq[:, 0:IT], T.xs[:, 0:IT], True, True), "dm%d" % b)
    for b in range(4):
        wait("v", "dm%d" % b)
        inc(v.tensor_tensor(T.xr[:, 4 * IT + b:8 * IT:4], T.xr[:, b:4 * IT:4], ybank[b][:, 0:IT], AluOpType.subtract), "rs")
    wait("v", "rs")
    inc(v.quantize_mx(T.xq[:, IT:2 * IT], T.xs[:, IT:2 * IT], T.xr[:, 4 * IT:8 * IT]), "rq")
    wait("g", "rq")
    for to in (helper, cores[mate]):
        send_xr(to, T.xq, T.xs, T.pq, T.ps, "pa")
    inc(g.iota(T.pm[:, :], [[0, 8], [1, 16]], 0, 0, allow_small_or_imprecise_dtypes=True), "kpm")

    wait("y", "ms")
    inc(sy.dma_start(T.nb[0:1, :, 0], T.bc[64:65, 0:128]), "nz", 16)
    wait("y", "nz")

    own = {rank: (T.xq, T.xs), mate: (T.pq, T.ps), peer: (T.fq, T.fs)}
    banks = {rank: (T.sc0, T.sc1), mate: (T.y0, T.y1), peer: (T.y2, T.y3)}

    def width(b):
        return len(near) if b == NB else len(sources(rank, b))

    def products(b):
        if b < NB:
            src = sources(rank, b)
            for r in src:
                expect("w%d" % r, 2 * n_off)
                wait("t", "w%d" % r)
            c0, n = Q * min(src), Q * len(src)
            for h in range(2):
                if b:
                    wait("t", ("saa%d", "sab%d")[h] % (b - 1))
                inc(pe.matmul_mx(banks[rank][h][:, 0:n], T.xq[:, 128 * h:128 * h + 128], T.xs[:, 128 * h:128 * h + 128],
                                 T.wq[:, c0:c0 + n], T.ws[:, c0:c0 + n], True, True), ("mma%d", "mmb%d")[h] % b)
            return
        expect("pa", 2 * n_on)
        expect("pf", 2 * n_off)
        for f in ("rs", "wqd", "rq", "saa%d" % (b - 1), "sab%d" % (b - 1)):
            wait("t", f)
        for s in (rank, mate, peer):
            if s != rank:
                wait("t", "pa" if s == mate else "pf")
            for h in range(2):
                inc(pe.matmul_mx(banks[s][h][:, 0:128], own[s][0][:, 128 * h:128 * h + 128], own[s][1][:, 128 * h:128 * h + 128],
                                 wcols[0], wcols[1], True, True), ("mma%d", "mmb%d")[h] % b)

    def over_queries(b):
        o, n = 512 * b, 128 * width(b)
        wait("v", "ms")
        for h in range(2):
            wait("v", ("mma%d", "mmb%d")[h] % b)
            parts = [(n, banks[rank][h], 0)] if b < NB else [(128, banks[s][h], 128 * l) for l, s in enumerate(near)]
            for w, bank, at in parts:
                q = o + n * h + at
                inc(v.tensor_tensor_scan(T.S[:, q:q + w], T.rst[:, 0:w], bank[:, 0:w], 0.0, ADD, MAX), ("saa%d", "sab%d")[h] % b)
        wait("t", "kid")
        if b:
            wait("t", "s2%d" % (b - 1))
        for h in range(2):
            wait("t", ("saa%d", "sab%d")[h] % b)
            inc(pe.transpose(T.tr[0:n // 16, 128 * h:128 * h + 128], T.S[:, o + n * h + 15:o + n * h + n:16], T.ident[:, :]), "trd%d" % b)

    def over_items(b):
        p, k = 256 * b, 8 * width(b)
        wait("v", "trd%d" % b)
        inc(v.tensor_tensor_scan(T.P[0:k, p:p + 256], T.tr[0:k, 0:256], T.neg[0:k, :], LOW, MAX, MAX), "s2%d" % b)
        wait("v", "s2%d" % b)
        inc(v.tensor_scalar(T.lt[0:k, 16 * b:16 * b + 16], T.P[0:k, p + 15:p + 256:16], T.P[0:k, p + 255:p + 256], 64.0,
                            AluOpType.is_lt, AluOpType.mult), "ltd%d" % b)
        wait("v", "ltd%d" % b)
        col = T.cc[0:k, 4 * b:4 * b + 1]
        inc(v.tensor_reduce(col, T.lt[0:k, 16 * b:16 * b + 16], AxisListType.X, ADD), "cb%d" % b)
        wait("v", "cb%d" % b)
        wait("v", "kpm")
        if b < NB:
            inc(v.tensor_scalar(T.bc[0:k, 128 * b:128 * b + 128], T.pm[0:k, :], col, None, ADD), "bcd%d" % b)
            if b < NB - 1:
                wait("y", "cb%d" % b)
                q = 8 * min(sources(rank, b))
                inc(sy.dma_start(T.nb[0:1, q:q + k, 0], col), "nd", 16)
        else:
            inc(v.tensor_scalar(T.bc[0:k, 128 * b:128 * b + 128], T.pm[0:k, :], 4.0, col, AluOpType.mult, ADD), "bcd%d" % b)
        wait("t", "bcd%d" % b)
        if b:
            wait("t", "ofd%d" % (b - 1))
        inc(pe.transpose(T.ob[:, 0:128], T.bc[:, 128 * b:128 * b + 128], T.ident[:, :]), "obd%d" % b)

    def offsets(b):
        k = 8 * width(b)
        wait("v", "obd%d" % b)
        if b < NB:
            for u in range(4):
                inc(v.tensor_scalar(T.of[:, 64 * b + u:64 * b + 4 * k:4], T.ob[:, 0:k], float(16 * u), None, ADD), "ofd%d" % b)
        else:
            inc(v.tensor_scalar(T.of[:, 64 * b:64 * b + k], T.ob[:, 0:k], 0.25, None, AluOpType.mult), "ofd%d" % b)
        wait("v", "ofd%d" % b)

    def lists(b, j):
        src = sources(rank, b)
        return 64 * b + 32 * sorted(src).index(src[j])

    def gather_x(b, j, q, a, e):
        i, f = 2 * b + j, lists(b, j)
        out, win = T.gt[:, 1024 * i + a:1024 * i + e], T.xr[:, 0:1024].indirect(T.of[:, f + a // 16:f + e // 16])
        wait(q, "ofd%d" % b)
        inc(v.tensor_copy(out, win) if q == "v" else act.activation(out, win, COPY), "gx%d" % i if q == "v" else "gr%d" % i)

    def gather_r(b, j):
        i, f = 2 * b + j, lists(b, j)
        wait("s", "ofd%d" % b)
        wait("s", "rs")
        inc(act.activation(T.gt[:, 1024 * i + 512:1024 * i + 1024], T.xr[:, 1024:2048].indirect(T.of[:, f:f + 32]), COPY), "gr%d" % i)

    def pack(b, j):
        i = 2 * b + j
        wait("v", "gx%d" % i)
        wait("v", "gr%d" % i)
        inc(v.quantize_mx(T.cq[:, 256 * i:256 * i + 256], T.cs[:, 256 * i:256 * i + 256], T.gt[:, 1024 * i:1024 * i + 1024]), "qz%d" % i)

    def ship(b, j):
        i, d = 2 * b + j, sources(rank, b)[j]
        wait("g", "qz%d" % i)
        if relayed(b, d, rank):
            send([helper], T.cq[:, 256 * i:256 * i + 256].bitcast(dt.uint8), T.cq[:, 256 * i:256 * i + 256].bitcast(dt.uint8), "hc%d" % i)
            send([helper], T.cs[:, 256 * i:256 * i + 256], T.cs[:, 256 * i:256 * i + 256], "hc%d" % i)
        else:
            send_c(cores[d], i, rank)

    products(0)
    over_queries(0)
    over_items(0)
    offsets(0)
    for b in range(NB):
        last = b == NB - 1
        items = range(width(b))
        for j in items:
            gather_r(b, j)
        if not last:
            gather_x(b, 1, "s", 256, 512)
        gather_x(b, 0, "v", 0, 512)
        if not last:
            products(b + 1)
            over_queries(b + 1)
        pack(b, 0)
        if not last:
            gather_x(b, 1, "v", 0, 256)
            pack(b, 1)
            over_items(b + 1)
            offsets(b + 1)
        for j in items:
            ship(b, j)
        if b == NB - 2:
            wait("g", "nd")
            send([cores[o] for k in range(NB - 1) for o in sources(rank, k)], T.nb[0], T.nl[rank], "nm", 1 << offe[-1])
            wait("g", "cb%d" % (NB - 1))
            send([cores[sources(rank, NB - 1)[0]]], T.cc[:, 4 * NB - 4:4 * NB - 3], T.nx[:, :], "nx")

    order = [(T.y1, "sab%d" % NB), (T.y2, "saa%d" % NB), (T.y3, "sab%d" % NB), (T.y0, "fb")]
    tiles = [(b, s) for b in range(NB) for s in owners(rank, b)]
    tiles.sort(key=lambda e: (2 + 2 * e[0]) if relayed(e[0], e[1], rank) else (0, 1, 3)[e[0]])

    def final(l):
        for p in l:
            s = tiles[p][1]
            bank = order[p % 4][0]
            expect("c%d" % s, 2 * n_off)
            wait("t", order[p][1] if p < 4 else "fy%d" % (p - 4))
            wait("t", "c%d" % s)
            pe.matmul_mx(bank[:, 0:128], wcols[0], wcols[1], T.lq[:, 256 * s:256 * s + 128], T.ls[:, 256 * s:256 * s + 128], True, False)
            inc(pe.matmul_mx(bank[:, 0:128], wcols[0], wcols[1], T.lq[:, 256 * s + 128:256 * s + 256],
                             T.ls[:, 256 * s + 128:256 * s + 256], False, True), "fm%d" % p)
            wait("s", "fm%d" % p)
            inc(act.activation(T.yt[:, 128 * s:128 * s + 128], bank[:, 0:128], COPY), "fy%d" % p)
            wait("s", "fy%d" % p)
            inc(act.dma_start(T.y[:, 128 * s:128 * s + 128], T.yt[:, 128 * s:128 * s + 128]), "sy", 16)

    b = NB
    products(b)
    over_queries(b)
    wide = (T.sc0, T.sc1, T.y0)
    for l, s in enumerate(near):
        wait("t", ("saa%d" if l != 1 else "sab%d") % b)
        pe.matmul_mx(wide[l][:, 0:IT], wcols[0], wcols[1], own[s][0][:, 0:IT], own[s][1][:, 0:IT], True, False)
        inc(pe.matmul_mx(wide[l][:, 0:IT], wcols[0], wcols[1], own[s][0][:, IT:2 * IT], own[s][1][:, IT:2 * IT], False, True), "fa%d" % l)
        wait("s", "fa%d" % l)
        inc(act.activation(T.ab[:, IT * l:IT * l + IT], wide[l][:, 0:IT], COPY), "fb")
    final(range(0, 2))
    over_items(b)
    wait("y", "cb%d" % b)
    inc(sy.dma_start(T.cht[duo[0]:duo[0] + 2, 0:8], T.cc[0:16, 4 * b:4 * b + 1]), "ct", 16)
    inc(sy.dma_start(T.cht[peer:peer + 1, 0:8], T.cc[16:24, 4 * b:4 * b + 1]), "ct", 16)
    offsets(b)
    wait("v", "fb")
    for l, s in enumerate(near):
        f0 = 64 * b + 8 * l
        inc(v.tensor_copy(T.yt[:, 128 * s:128 * s + 128], T.ab[:, IT * l:IT * l + IT].indirect(T.of[:, f0:f0 + 8])), "fg")
    wait("s", "fg")
    inc(act.dma_start(T.y[:, 128 * duo[0]:128 * duo[0] + 256], T.yt[:, 128 * duo[0]:128 * duo[0] + 256]), "sy", 16)
    inc(act.dma_start(T.y[:, 128 * peer:128 * peer + 128], T.yt[:, 128 * peer:128 * peer + 128]), "sy", 16)
    final(range(2, NI))

    expect("nm", sum(len(owners(rank, k)) for k in range(NB - 1)))
    expect("nx", n_off)
    wait("y", "nm")
    for k in range(NB - 1):
        s = owners(rank, k)[0]
        inc(sy.dma_start(T.cht[s:s + 2, 0:8], T.nl[s:s + 2, 8 * rank:8 * rank + 8, 0]), "ct", 16)
    wait("v", "ct")
    inc(v.transpose(T.chu[:, :], T.cht[:, :]), "ch1")
    wait("v", "ch1")
    inc(v.tensor_scalar(T.cho[0:8, 0:8], T.chu[0:8, 0:8], 1.0 / 64.0, None, AluOpType.mult), "ch2")
    wait("v", "ch2")
    wait("v", "nx")
    s = owners(rank, NB - 1)[0]
    inc(v.tensor_scalar(T.cho[0:8, s:s + 1], T.nx[0:8, :], 1.0 / 64.0, None, AluOpType.mult), "ch3")
    wait("y", "ch3")
    inc(sy.dma_start(T.ch[:, :], T.cho[0:8, 0:8]), "sc", 16)
    finish()
